import numpy as np, ml_dtypes
CORES = [2,3,42,43,82,83,122,123]
N = 8
import mx_ref
NC, G = 256, 2
C = np.float32(0.043)
BF = ml_dtypes.bfloat16
def cut(t, i, w=512):
    return t[:, w * i:w * i + w]
def tile(rs):
    return np.stack(rs, axis=2).reshape(128, -1).astype(BF)
def layer(w, X):
    out = []
    for i in range(G):
        for t in range(len(X)):
            p = mx_ref.matmul(mx_ref.quantize(cut(w, len(X) * i + t)), X[t])
            z = p if t == 0 else z + p
        out.append(z)
    return out
def act(Z):
    return [np.maximum(s * z, 0) * C for z in Z for s in (1, -1)]
def setup_inputs(rng):
    def f(*shape):
        return mx_ref.flush((rng.standard_normal(shape, dtype=np.float32) * np.exp2(rng.integers(-2, 3, shape[:-1] + (1,)))).astype(BF))
    return {"x": f(N, 128, 4 * NC), "w1": f(N, 128, G * 512), "w2": f(N, 128, 512)}
def setup_inputs_blocks(rng):
    d = setup_inputs(rng)
    for k in ("x", "w1", "w2"): d[k] = mx_ref.spread(d[k], rng, 2)
    return d
def setup_inputs_wide(rng):
    d = setup_inputs(rng)
    for k in ("x", "w1", "w2"): d[k] = mx_ref.flush((d[k].astype(np.float32) * np.exp2(rng.integers(-6, 7, (N, 1, 1))).astype(np.float32)).astype(BF))
    return d
def reference(x, w1, w2):
    X = [mx_ref.quantize(x[j]) for j in range(N)]
    y = np.zeros((N, 128, NC), np.float32)
    for c in range(N):
        for r in range(N):
            p = mx_ref.matmul(mx_ref.quantize(w2[r]), mx_ref.quantize(tile(act(layer(w1[r], [X[c]])))))
            y[c] = p if r == 0 else y[c] + p
    return {"y": y}

@@ -1,0 +1,216 @@
+from concourse.bass import DstId, RemoteDMATransfer
+from concourse.mybir import dt, AluOpType, ActivationFunctionType
+
+N = 8
+NC = 256
+WC = 384
+CSC = 0.043
+TWO_DIE = False
+FWD_KIND = {1: "hi", 2: "hi", 3: "all"}
+ROUND_PARTS = {1: ("C", "S"), 2: ("C", "S"), 3: ("S", "A", "B")}
+DUP = ()
+
+PARTS = {"A": ("q", 0, 256), "B": ("q", 256, 384), "C": ("q", 0, 384), "S": ("s", 0, 384)}
+
+SCRATCH = {
+    "wb": ("sbuf", [128, 1536], "bfloat16"),
+    "xb": ("sbuf", [128, 1024], "bfloat16"),
+    "xq": ("sbuf", [128, NC], "float8_e4m3fn_x4"),
+    "xs": ("sbuf", [128, NC], "uint8"),
+    "wq": ("sbuf", [128, N * WC], "float8_e4m3fn_x4"),
+    "ws": ("sbuf", [128, N * WC], "uint8"),
+    "h": ("sbuf", [128, N * 4 * NC], "bfloat16"),
+    "hq": ("sbuf", [128, N * NC], "float8_e4m3fn_x4"),
+    "hs": ("sbuf", [128, N * NC], "uint8"),
+    "yo": ("sbuf", [128, NC], "float32"),
+    "zp": ("psum", [128, 512 * 6], "float32"),
+    "yp": ("psum", [128, 512], "float32"),
+}
+SEMAPHORES = (["ldw1", "ldw2", "ldx", "qw1", "qw2", "qx", "sent", "ydone", "ycp", "st"]
+              + ["a%d%s" % (r, p) for r in range(N) for p in sorted(PARTS)]
+              + ["%s%d" % (s, k) for s in ("za", "zb", "ha", "hq") for k in range(N)])
+
+
+def popcount(m):
+    return bin(m).count("1")
+
+
+def make_plan(cores, topo):
+    chips = []
+    for c in cores:
+        if topo.chip(c) not in chips:
+            chips.append(topo.chip(c))
+    nch = len(chips)
+    members = {ch: [c for c in cores if topo.chip(c) == ch] for ch in chips}
+    everyone = range(topo.CHIPS * topo.CORES_PER_CHIP)
+    sends, gets, order = {}, {}, {}
+
+    def pick(u, dsts, kind):
+        m = -1
+        for d in dsts:
+            m &= topo.mask(u, d)
+        if kind == "hi":
+            away = [c for c in cores if topo.chip(c) != topo.chip(u)][0]
+            m &= ~topo.mask(u, away)
+        return m
+
+    def add(u, r, part, dsts, kind):
+        m = pick(u, dsts, kind)
+        sends.setdefault(u, []).append((r, part, tuple(dsts), m))
+        for d in dsts:
+            gets.setdefault(d, {}).setdefault(r, []).append((part, popcount(m)))
+
+    def dest(i, j, k):
+        mem = members[chips[(i + k) % nch]]
+        return mem[j % len(mem)]
+
+    direct = set()
+
+    def out(u, r, i, j, k, part):
+        if (k, part) in DUP:
+            direct.add((r, part, chips[(i + k) % nch]))
+            add(u, r, part, members[chips[(i + k) % nch]], "off")
+        else:
+            add(u, r, part, [dest(i, j, k)], "off")
+
+    for i, ch in enumerate(chips):
+        away = [c for c in cores if topo.chip(c) != ch]
+        spare = [c for c in everyone if topo.chip(c) == ch and c not in cores
+                 and topo.die(c) != topo.die(members[ch][0]) and all(topo.may_write(c, d) for d in away)]
+        for j, u in enumerate(members[ch]):
+            r = cores.index(u)
+            sibs = [c for c in members[ch] if c != u]
+            if TWO_DIE:
+                hlp = spare[j]
+                out(u, r, i, j, 1, "A")
+                add(u, r, "S", [hlp], "hi")
+                add(u, r, "B", [hlp], "hi")
+                for k in range(2, nch):
+                    out(u, r, i, j, k, "A")
+                add(u, r, "C", sibs, "hi")
+                add(u, r, "S", sibs, "hi")
+                for k in range(1, nch):
+                    out(hlp, r, i, j, k, "S")
+                    out(hlp, r, i, j, k, "B")
+            else:
+                for k in range(1, nch):
+                    for part in ROUND_PARTS[k]:
+                        out(u, r, i, j, k, part)
+                    if k == 1:
+                        add(u, r, "C", sibs, "hi")
+                        add(u, r, "S", sibs, "hi")
+    for i, ch in enumerate(chips):
+        for j, v in enumerate(members[ch]):
+            sibs = [c for c in members[ch] if c != v]
+            order[v] = [cores.index(v)] + [cores.index(c) for c in sibs]
+            for k in range(1, nch):
+                src = members[chips[(i - k) % nch]]
+                r = cores.index(src[j])
+                for part, _ in list(gets[v][r]):
+                    if (r, part, ch) not in direct:
+                        add(v, r, part, sibs, FWD_KIND[k])
+                order[v] += [r] + [cores.index(c) for c in src if c != src[j]]
+    return sends, gets, order
+
+
+def view(T, r, part):
+    kind, a, b = PARTS[part]
+    if kind == "q":
+        return T.wq[:, WC * r + a:WC * r + b].bitcast(dt.uint8)
+    return T.ws[:, WC * r + a:WC * r + b]
+
+
+def rank_program(g, core, T, topo):
+    cores = list(T.cores)
+    sends, gets, order = make_plan(cores, topo)
+    rank = T.rank_of(core)
+    S = T.sem
+
+    if rank is not None:
+        compute(g, T, rank, order[core], gets[core])
+
+    total = 0
+    for r, part, dsts, m in sends.get(core, []):
+        if r == rank:
+            if part != "B":
+                g.wait_ge(S.qw1, 1)
+            if part != "A":
+                g.wait_ge(S.qw2, 1)
+        else:
+            g.wait_ge(S["a%d%s" % (r, part)], dict(gets[core][r])[part])
+        v = view(T, r, part)
+        sem = S["a%d%s" % (r, part)]
+        if len(dsts) == 1:
+            rid, pid, _ = topo.addr(dsts[0])
+            g.remote_dma(v, v, sem, S.sent, pid, rid, m)
+        else:
+            ids = [DstId(rid=topo.addr(d)[0], pnc=topo.addr(d)[1]) for d in dsts]
+            g.remote_dma_fused([RemoteDMATransfer(dst_ids=ids, dma_engine_mask=m, remote_sem=sem,
+                                                  srcs=[v], dsts=[v] * len(dsts))], local_sem=S.sent)
+        total += popcount(m)
+    if total:
+        g.wait_ge(S.sent, total)
+
+
+def compute(g, T, rank, order, gets):
+    S = T.sem
+    t, v, sc = g.tensor, g.vector, g.scalar
+    o = WC * rank
+    g.sync.dma_start(T.wb[:, 0:1024], T.w1[:, :]).then_inc(S.ldw1, 16)
+    sc.dma_start(T.wb[:, 1024:1536], T.w2[:, :]).then_inc(S.ldw2, 16)
+    g.sync.dma_start(T.xb[:], T.x[:, :]).then_inc(S.ldx, 16)
+    v.wait_ge(S.ldw1, 16)
+    v.quantize_mx(T.wq[:, o:o + 256], T.ws[:, o:o + 256], T.wb[:, 0:1024]).then_inc(S.qw1, 1)
+    v.wait_ge(S.ldw2, 16)
+    v.quantize_mx(T.wq[:, o + 256:o + 384], T.ws[:, o + 256:o + 384], T.wb[:, 1024:1536]).then_inc(S.qw2, 1)
+    v.wait_ge(S.ldx, 16)
+    v.quantize_mx(T.xq[:], T.xs[:], T.xb[:]).then_inc(S.qx, 1)
+
+    def zmm(k):
+        r = order[k]
+        if r == rank:
+            for s in (S.qw1, S.qw2, S.qx):
+                t.wait_ge(s, 1)
+        else:
+            for part, n in gets[r]:
+                if part != "B":
+                    t.wait_ge(S["a%d%s" % (r, part)], n)
+        if k >= 3:
+            t.wait_ge(S["ha%d" % (k - 3)], 4)
+        for i, s in enumerate(("za", "zb")):
+            b = 1024 * (k % 3) + 512 * i
+            w = WC * r + 128 * i
+            t.matmul_mx(T.zp[:, b:b + NC], T.wq[:, w:w + 128], T.ws[:, w:w + 128], T.xq[:], T.xs[:],
+                        True, True).then_inc(S["%s%d" % (s, k)], 1)
+
+    zmm(0)
+    for k in range(N):
+        if k + 1 < N:
+            zmm(k + 1)
+        b = 1024 * (k % 3)
+        hb = 4 * NC * k
+        ha = S["ha%d" % k]
+        z0, z1 = T.zp[:, b:b + NC], T.zp[:, b + 512:b + 512 + NC]
+        v.wait_ge(S["za%d" % k], 1)
+        v.tensor_scalar(T.h[:, hb + 0:hb + 4 * NC:4], z0, 0.0, CSC, AluOpType.max, AluOpType.mult).then_inc(ha, 1)
+        v.tensor_scalar(T.h[:, hb + 1:hb + 4 * NC:4], z0, -CSC, 0.0, AluOpType.mult, AluOpType.max).then_inc(ha, 1)
+        sc.wait_ge(S["zb%d" % k], 1)
+        sc.activation(T.h[:, hb + 2:hb + 4 * NC:4], z1, ActivationFunctionType.Relu, scale=CSC).then_inc(ha, 1)
+        sc.activation(T.h[:, hb + 3:hb + 4 * NC:4], z1, ActivationFunctionType.Relu, scale=-CSC).then_inc(ha, 1)
+        v.wait_ge(ha, 4)
+        v.quantize_mx(T.hq[:, NC * k:NC * k + NC], T.hs[:, NC * k:NC * k + NC],
+                      T.h[:, hb:hb + 4 * NC]).then_inc(S["hq%d" % k], 1)
+        w = WC * order[k] + 256
+        for part, n in gets.get(order[k], ()):
+            if part == "B":
+                t.wait_ge(S["a%d%s" % (order[k], part)], n)
+        t.wait_ge(S["hq%d" % k], 1)
+        mm = t.matmul_mx(T.yp[:, 0:NC], T.wq[:, w:w + 128], T.ws[:, w:w + 128],
+                         T.hq[:, NC * k:NC * k + NC], T.hs[:, NC * k:NC * k + NC], k == 0, k == N - 1)
+        if k == N - 1:
+            mm.then_inc(S.ydone, 1)
+    v.wait_ge(S.ydone, 1)
+    v.tensor_copy(T.yo[:], T.yp[:, 0:NC]).then_inc(S.ycp, 1)
+    g.sync.wait_ge(S.ycp, 1)
+    g.sync.dma_start(T.y[:, :], T.yo[:]).then_inc(S.st, 16)
+    g.sync.wait_ge(S.st, 16)

@@ -5,12 +5,12 @@ N = 8
 NC = 256
 WC = 384
 CSC = 0.043
-TWO_DIE = False
-FWD_KIND = {1: "hi", 2: "hi", 3: "all"}
-ROUND_PARTS = {1: ("C", "S"), 2: ("C", "S"), 3: ("S", "A", "B")}
-DUP = ()
 
 PARTS = {"A": ("q", 0, 256), "B": ("q", 256, 384), "C": ("q", 0, 384), "S": ("s", 0, 384)}
+OWN = [("B", "hlp", "off"), ("A", 1, "off"), ("S", 1, "off"), ("C", "sib", "hi"), ("S", "sib", "hi"),
+       ("A", 2, "off"), ("S", 2, "off"), ("A", 3, "off"), ("S", 3, "off")]
+RELAY = [("B", 1, "off"), ("B", 2, "off"), ("B", 3, "off")]
+FWD = [(1, "A", "hi"), (1, "S", "hi"), (2, "A", "hi"), (2, "S", "hi"), (3, "A", "all"), (3, "S", "all")]
 
 SCRATCH = {
     "wb": ("sbuf", [128, 1536], "bfloat16"),
@@ -49,9 +49,11 @@ def make_plan(cores, topo):
         m = -1
         for d in dsts:
             m &= topo.mask(u, d)
+        away = topo.mask(u, [c for c in cores if topo.chip(c) != topo.chip(u)][0])
         if kind == "hi":
-            away = [c for c in cores if topo.chip(c) != topo.chip(u)][0]
-            m &= ~topo.mask(u, away)
+            m &= ~away
+        elif kind != "all":
+            m &= away
         return m
 
     def add(u, r, part, dsts, kind):
@@ -64,52 +66,30 @@ def make_plan(cores, topo):
         mem = members[chips[(i + k) % nch]]
         return mem[j % len(mem)]
 
-    direct = set()
-
-    def out(u, r, i, j, k, part):
-        if (k, part) in DUP:
-            direct.add((r, part, chips[(i + k) % nch]))
-            add(u, r, part, members[chips[(i + k) % nch]], "off")
-        else:
-            add(u, r, part, [dest(i, j, k)], "off")
-
     for i, ch in enumerate(chips):
         away = [c for c in cores if topo.chip(c) != ch]
         spare = [c for c in everyone if topo.chip(c) == ch and c not in cores
                  and topo.die(c) != topo.die(members[ch][0]) and all(topo.may_write(c, d) for d in away)]
         for j, u in enumerate(members[ch]):
             r = cores.index(u)
-            sibs = [c for c in members[ch] if c != u]
-            if TWO_DIE:
-                hlp = spare[j]
-                out(u, r, i, j, 1, "A")
-                add(u, r, "S", [hlp], "hi")
-                add(u, r, "B", [hlp], "hi")
-                for k in range(2, nch):
-                    out(u, r, i, j, k, "A")
-                add(u, r, "C", sibs, "hi")
-                add(u, r, "S", sibs, "hi")
-                for k in range(1, nch):
-                    out(hlp, r, i, j, k, "S")
-                    out(hlp, r, i, j, k, "B")
-            else:
-                for k in range(1, nch):
-                    for part in ROUND_PARTS[k]:
-                        out(u, r, i, j, k, part)
-                    if k == 1:
-                        add(u, r, "C", sibs, "hi")
-                        add(u, r, "S", sibs, "hi")
+            for part, to, kind in OWN:
+                if to == "sib":
+                    add(u, r, part, [c for c in members[ch] if c != u], kind)
+                elif to == "hlp":
+                    add(u, r, part, [spare[j]], kind)
+                else:
+                    add(u, r, part, [dest(i, j, to)], kind)
+            for part, k, kind in RELAY:
+                add(spare[j], r, part, members[chips[(i + k) % nch]], kind)
     for i, ch in enumerate(chips):
         for j, v in enumerate(members[ch]):
             sibs = [c for c in members[ch] if c != v]
             order[v] = [cores.index(v)] + [cores.index(c) for c in sibs]
+            for k, part, kind in FWD:
+                add(v, cores.index(members[chips[(i - k) % nch]][j]), part, sibs, kind)
             for k in range(1, nch):
                 src = members[chips[(i - k) % nch]]
-                r = cores.index(src[j])
-                for part, _ in list(gets[v][r]):
-                    if (r, part, ch) not in direct:
-                        add(v, r, part, sibs, FWD_KIND[k])
-                order[v] += [r] + [cores.index(c) for c in src if c != src[j]]
+                order[v] += [cores.index(src[j])] + [cores.index(c) for c in src if c != src[j]]
     return sends, gets, order
 
 
@@ -156,13 +136,13 @@ def compute(g, T, rank, order, gets):
     S = T.sem
     t, v, sc = g.tensor, g.vector, g.scalar
     o = WC * rank
-    g.sync.dma_start(T.wb[:, 0:1024], T.w1[:, :]).then_inc(S.ldw1, 16)
     sc.dma_start(T.wb[:, 1024:1536], T.w2[:, :]).then_inc(S.ldw2, 16)
+    g.sync.dma_start(T.wb[:, 0:1024], T.w1[:, :]).then_inc(S.ldw1, 16)
     g.sync.dma_start(T.xb[:], T.x[:, :]).then_inc(S.ldx, 16)
-    v.wait_ge(S.ldw1, 16)
-    v.quantize_mx(T.wq[:, o:o + 256], T.ws[:, o:o + 256], T.wb[:, 0:1024]).then_inc(S.qw1, 1)
     v.wait_ge(S.ldw2, 16)
     v.quantize_mx(T.wq[:, o + 256:o + 384], T.ws[:, o + 256:o + 384], T.wb[:, 1024:1536]).then_inc(S.qw2, 1)
+    v.wait_ge(S.ldw1, 16)
+    v.quantize_mx(T.wq[:, o:o + 256], T.ws[:, o:o + 256], T.wb[:, 0:1024]).then_inc(S.qw1, 1)
     v.wait_ge(S.ldx, 16)
     v.quantize_mx(T.xq[:], T.xs[:], T.xb[:]).then_inc(S.qx, 1)
 

@@ -6,11 +6,17 @@ NC = 256
 WC = 384
 CSC = 0.043
 
-PARTS = {"A": ("q", 0, 256), "B": ("q", 256, 384), "C": ("q", 0, 384), "S": ("s", 0, 384)}
-OWN = [("B", "hlp", "off"), ("A", 1, "off"), ("S", 1, "off"), ("C", "sib", "hi"), ("S", "sib", "hi"),
-       ("A", 2, "off"), ("S", 2, "off"), ("A", 3, "off"), ("S", 3, "off")]
-RELAY = [("B", 1, "off"), ("B", 2, "off"), ("B", 3, "off")]
-FWD = [(1, "A", "hi"), (1, "S", "hi"), (2, "A", "hi"), (2, "S", "hi"), (3, "A", "all"), (3, "S", "all")]
+PARTS = {"A0": ("q", 0, 128), "A1": ("q", 128, 256), "A": ("q", 0, 256), "B": ("q", 256, 384), "C": ("q", 0, 384),
+         "S": ("s", 0, 384)}
+FROM_W1 = ("A0", "A1", "A", "C", "S")
+FROM_W2 = ("B", "C", "S")
+OWN = [("B", "hlp", "off"), ("A", 1, "off"), ("S", 1, "off"),
+       ("A1", "hlp", "hi"), ("S", "hlp", "hi"),
+       ("A", 2, "off"), ("S", 2, "off"), ("A0", 3, "off"), ("C", "sib", "hi"), ("S", "sib", "hi")]
+RELAY = [("B", 1, "one", "off"), ("B", 2, "one", "off"), ("A1", 3, "one", "off"), ("S", 3, "one", "off"),
+         ("B", 3, "one", "off")]
+FWD = [(1, "A", "hi"), (1, "S", "hi"), (1, "B", "hi"), (2, "A", "hi"), (2, "S", "hi"), (2, "B", "hi"),
+       (3, "A1", "hi"), (3, "S", "hi"), (3, "A0", "all"), (3, "B", "all")]
 
 SCRATCH = {
     "wb": ("sbuf", [128, 1536], "bfloat16"),
@@ -79,8 +85,8 @@ def make_plan(cores, topo):
                     add(u, r, part, [spare[j]], kind)
                 else:
                     add(u, r, part, [dest(i, j, to)], kind)
-            for part, k, kind in RELAY:
-                add(spare[j], r, part, members[chips[(i + k) % nch]], kind)
+            for part, k, who, kind in RELAY:
+                add(spare[j], r, part, members[chips[(i + k) % nch]] if who == "both" else [dest(i, j, k)], kind)
     for i, ch in enumerate(chips):
         for j, v in enumerate(members[ch]):
             sibs = [c for c in members[ch] if c != v]
@@ -112,9 +118,9 @@ def rank_program(g, core, T, topo):
     total = 0
     for r, part, dsts, m in sends.get(core, []):
         if r == rank:
-            if part != "B":
+            if part in FROM_W1:
                 g.wait_ge(S.qw1, 1)
-            if part != "A":
+            if part in FROM_W2:
                 g.wait_ge(S.qw2, 1)
         else:
             g.wait_ge(S["a%d%s" % (r, part)], dict(gets[core][r])[part])
@@ -146,49 +152,69 @@ def compute(g, T, rank, order, gets):
     v.wait_ge(S.ldx, 16)
     v.quantize_mx(T.xq[:], T.xs[:], T.xb[:]).then_inc(S.qx, 1)
 
-    def zmm(k):
+    def there(k, names):
         r = order[k]
         if r == rank:
             for s in (S.qw1, S.qw2, S.qx):
                 t.wait_ge(s, 1)
-        else:
-            for part, n in gets[r]:
-                if part != "B":
-                    t.wait_ge(S["a%d%s" % (r, part)], n)
+        for part, n in gets.get(r, ()):
+            if part in names:
+                t.wait_ge(S["a%d%s" % (r, part)], n)
+
+    def zmm(k, i):
+        there(k, ("A0", "A", "C", "S") if i == 0 else ("A1", "A", "C", "S"))
         if k >= 3:
             t.wait_ge(S["ha%d" % (k - 3)], 4)
-        for i, s in enumerate(("za", "zb")):
-            b = 1024 * (k % 3) + 512 * i
-            w = WC * r + 128 * i
-            t.matmul_mx(T.zp[:, b:b + NC], T.wq[:, w:w + 128], T.ws[:, w:w + 128], T.xq[:], T.xs[:],
-                        True, True).then_inc(S["%s%d" % (s, k)], 1)
+        b = 1024 * (k % 3) + 512 * i
+        w = WC * order[k] + 128 * i
+        t.matmul_mx(T.zp[:, b:b + NC], T.wq[:, w:w + 128], T.ws[:, w:w + 128], T.xq[:], T.xs[:],
+                    True, True).then_inc(S["%s%d" % ("za" if i == 0 else "zb", k)], 1)
 
-    zmm(0)
-    for k in range(N):
-        if k + 1 < N:
-            zmm(k + 1)
-        b = 1024 * (k % 3)
-        hb = 4 * NC * k
-        ha = S["ha%d" % k]
-        z0, z1 = T.zp[:, b:b + NC], T.zp[:, b + 512:b + 512 + NC]
-        v.wait_ge(S["za%d" % k], 1)
-        v.tensor_scalar(T.h[:, hb + 0:hb + 4 * NC:4], z0, 0.0, CSC, AluOpType.max, AluOpType.mult).then_inc(ha, 1)
-        v.tensor_scalar(T.h[:, hb + 1:hb + 4 * NC:4], z0, -CSC, 0.0, AluOpType.mult, AluOpType.max).then_inc(ha, 1)
-        sc.wait_ge(S["zb%d" % k], 1)
-        sc.activation(T.h[:, hb + 2:hb + 4 * NC:4], z1, ActivationFunctionType.Relu, scale=CSC).then_inc(ha, 1)
-        sc.activation(T.h[:, hb + 3:hb + 4 * NC:4], z1, ActivationFunctionType.Relu, scale=-CSC).then_inc(ha, 1)
-        v.wait_ge(ha, 4)
-        v.quantize_mx(T.hq[:, NC * k:NC * k + NC], T.hs[:, NC * k:NC * k + NC],
-                      T.h[:, hb:hb + 4 * NC]).then_inc(S["hq%d" % k], 1)
-        w = WC * order[k] + 256
-        for part, n in gets.get(order[k], ()):
-            if part == "B":
-                t.wait_ge(S["a%d%s" % (order[k], part)], n)
+    def ymm(k):
+        there(k, ("B", "C", "S"))
         t.wait_ge(S["hq%d" % k], 1)
+        w = WC * order[k] + 256
         mm = t.matmul_mx(T.yp[:, 0:NC], T.wq[:, w:w + 128], T.ws[:, w:w + 128],
                          T.hq[:, NC * k:NC * k + NC], T.hs[:, NC * k:NC * k + NC], k == 0, k == N - 1)
         if k == N - 1:
             mm.then_inc(S.ydone, 1)
+
+    for k in range(N - 2):
+        zmm(k, 0)
+        zmm(k, 1)
+        if k >= 3:
+            ymm(k - 3)
+    zmm(N - 2, 1)
+    ymm(N - 5)
+    zmm(N - 1, 1)
+    ymm(N - 4)
+    zmm(N - 2, 0)
+    zmm(N - 1, 0)
+    ymm(N - 3)
+    ymm(N - 2)
+    ymm(N - 1)
+
+    def hcol(k, b):
+        return T.h[:, 4 * NC * k + b:4 * NC * (k + 1):4]
+
+    def zbank(k, i):
+        b = 1024 * (k % 3) + 512 * i
+        return T.zp[:, b:b + NC]
+
+    for k, i in [(k, 1) for k in range(N)] + [(N - 1, 0)]:
+        sc.wait_ge(S["%s%d" % ("za" if i == 0 else "zb", k)], 1)
+        sc.activation(hcol(k, 2 * i), zbank(k, i), ActivationFunctionType.Relu, scale=CSC).then_inc(S["ha%d" % k], 1)
+        sc.activation(hcol(k, 2 * i + 1), zbank(k, i), ActivationFunctionType.Relu,
+                      scale=-CSC).then_inc(S["ha%d" % k], 1)
+    for k in range(N):
+        ha = S["ha%d" % k]
+        if k < N - 1:
+            v.wait_ge(S["za%d" % k], 1)
+            v.tensor_scalar(hcol(k, 0), zbank(k, 0), 0.0, CSC, AluOpType.max, AluOpType.mult).then_inc(ha, 1)
+            v.tensor_scalar(hcol(k, 1), zbank(k, 0), -CSC, 0.0, AluOpType.mult, AluOpType.max).then_inc(ha, 1)
+        v.wait_ge(ha, 4)
+        v.quantize_mx(T.hq[:, NC * k:NC * k + NC], T.hs[:, NC * k:NC * k + NC],
+                      T.h[:, 4 * NC * k:4 * NC * (k + 1)]).then_inc(S["hq%d" % k], 1)
     v.wait_ge(S.ydone, 1)
     v.tensor_copy(T.yo[:], T.yp[:, 0:NC]).then_inc(S.ycp, 1)
     g.sync.wait_ge(S.ycp, 1)

from concourse.bass import DstId, RemoteDMATransfer
from concourse.mybir import dt, AluOpType, ActivationFunctionType

N = 8
NC = 256
WC = 384
CSC = 0.043

PARTS = {"A0": ("q", 0, 128), "A1": ("q", 128, 256), "A": ("q", 0, 256), "B": ("q", 256, 384), "C": ("q", 0, 384),
         "S": ("s", 0, 384)}
FROM_W1 = ("A0", "A1", "A", "C", "S")
FROM_W2 = ("B", "C", "S")
OWN = [("B", "hlp", "off"), ("A", 1, "off"), ("S", 1, "off"),
       ("A1", "hlp", "hi"), ("S", "hlp", "hi"),
       ("A", 2, "off"), ("S", 2, "off"), ("A0", 3, "off"), ("C", "sib", "hi"), ("S", "sib", "hi")]
RELAY = [("B", 1, "one", "off"), ("B", 2, "one", "off"), ("A1", 3, "one", "off"), ("S", 3, "one", "off"),
         ("B", 3, "one", "off")]
FWD = [(1, "A", "hi"), (1, "S", "hi"), (1, "B", "hi"), (2, "A", "hi"), (2, "S", "hi"), (2, "B", "hi"),
       (3, "A1", "hi"), (3, "S", "hi"), (3, "A0", "all"), (3, "B", "all")]

SCRATCH = {
    "wb": ("sbuf", [128, 1536], "bfloat16"),
    "xb": ("sbuf", [128, 1024], "bfloat16"),
    "xq": ("sbuf", [128, NC], "float8_e4m3fn_x4"),
    "xs": ("sbuf", [128, NC], "uint8"),
    "wq": ("sbuf", [128, N * WC], "float8_e4m3fn_x4"),
    "ws": ("sbuf", [128, N * WC], "uint8"),
    "h": ("sbuf", [128, N * 4 * NC], "bfloat16"),
    "hq": ("sbuf", [128, N * NC], "float8_e4m3fn_x4"),
    "hs": ("sbuf", [128, N * NC], "uint8"),
    "yo": ("sbuf", [128, NC], "float32"),
    "zp": ("psum", [128, 512 * 6], "float32"),
    "yp": ("psum", [128, 512], "float32"),
}
SEMAPHORES = (["ldw1", "ldw2", "ldx", "qw1", "qw2", "qx", "sent", "ydone", "ycp", "st"]
              + ["a%d%s" % (r, p) for r in range(N) for p in sorted(PARTS)]
              + ["%s%d" % (s, k) for s in ("za", "zb", "ha", "hq") for k in range(N)])


def popcount(m):
    return bin(m).count("1")


def make_plan(cores, topo):
    chips = []
    for c in cores:
        if topo.chip(c) not in chips:
            chips.append(topo.chip(c))
    nch = len(chips)
    members = {ch: [c for c in cores if topo.chip(c) == ch] for ch in chips}
    everyone = range(topo.CHIPS * topo.CORES_PER_CHIP)
    sends, gets, order = {}, {}, {}

    def pick(u, dsts, kind):
        m = -1
        for d in dsts:
            m &= topo.mask(u, d)
        away = topo.mask(u, [c for c in cores if topo.chip(c) != topo.chip(u)][0])
        if kind == "hi":
            m &= ~away
        elif kind != "all":
            m &= away
        return m

    def add(u, r, part, dsts, kind):
        m = pick(u, dsts, kind)
        sends.setdefault(u, []).append((r, part, tuple(dsts), m))
        for d in dsts:
            gets.setdefault(d, {}).setdefault(r, []).append((part, popcount(m)))

    def dest(i, j, k):
        mem = members[chips[(i + k) % nch]]
        return mem[j % len(mem)]

    for i, ch in enumerate(chips):
        away = [c for c in cores if topo.chip(c) != ch]
        spare = [c for c in everyone if topo.chip(c) == ch and c not in cores
                 and topo.die(c) != topo.die(members[ch][0]) and all(topo.may_write(c, d) for d in away)]
        for j, u in enumerate(members[ch]):
            r = cores.index(u)
            for part, to, kind in OWN:
                if to == "sib":
                    add(u, r, part, [c for c in members[ch] if c != u], kind)
                elif to == "hlp":
                    add(u, r, part, [spare[j]], kind)
                else:
                    add(u, r, part, [dest(i, j, to)], kind)
            for part, k, who, kind in RELAY:
                add(spare[j], r, part, members[chips[(i + k) % nch]] if who == "both" else [dest(i, j, k)], kind)
    for i, ch in enumerate(chips):
        for j, v in enumerate(members[ch]):
            sibs = [c for c in members[ch] if c != v]
            order[v] = [cores.index(v)] + [cores.index(c) for c in sibs]
            for k, part, kind in FWD:
                add(v, cores.index(members[chips[(i - k) % nch]][j]), part, sibs, kind)
            for k in range(1, nch):
                src = members[chips[(i - k) % nch]]
                order[v] += [cores.index(src[j])] + [cores.index(c) for c in src if c != src[j]]
    return sends, gets, order


def view(T, r, part):
    kind, a, b = PARTS[part]
    if kind == "q":
        return T.wq[:, WC * r + a:WC * r + b].bitcast(dt.uint8)
    return T.ws[:, WC * r + a:WC * r + b]


def rank_program(g, core, T, topo):
    cores = list(T.cores)
    sends, gets, order = make_plan(cores, topo)
    rank = T.rank_of(core)
    S = T.sem

    if rank is not None:
        compute(g, T, rank, order[core], gets[core])

    total = 0
    for r, part, dsts, m in sends.get(core, []):
        if r == rank:
            if part in FROM_W1:
                g.wait_ge(S.qw1, 1)
            if part in FROM_W2:
                g.wait_ge(S.qw2, 1)
        else:
            g.wait_ge(S["a%d%s" % (r, part)], dict(gets[core][r])[part])
        v = view(T, r, part)
        sem = S["a%d%s" % (r, part)]
        if len(dsts) == 1:
            rid, pid, _ = topo.addr(dsts[0])
            g.remote_dma(v, v, sem, S.sent, pid, rid, m)
        else:
            ids = [DstId(rid=topo.addr(d)[0], pnc=topo.addr(d)[1]) for d in dsts]
            g.remote_dma_fused([RemoteDMATransfer(dst_ids=ids, dma_engine_mask=m, remote_sem=sem,
                                                  srcs=[v], dsts=[v] * len(dsts))], local_sem=S.sent)
        total += popcount(m)
    if total:
        g.wait_ge(S.sent, total)


def compute(g, T, rank, order, gets):
    S = T.sem
    t, v, sc = g.tensor, g.vector, g.scalar
    o = WC * rank
    sc.dma_start(T.wb[:, 1024:1536], T.w2[:, :]).then_inc(S.ldw2, 16)
    g.sync.dma_start(T.wb[:, 0:1024], T.w1[:, :]).then_inc(S.ldw1, 16)
    g.sync.dma_start(T.xb[:], T.x[:, :]).then_inc(S.ldx, 16)
    v.wait_ge(S.ldw2, 16)
    v.quantize_mx(T.wq[:, o + 256:o + 384], T.ws[:, o + 256:o + 384], T.wb[:, 1024:1536]).then_inc(S.qw2, 1)
    v.wait_ge(S.ldw1, 16)
    v.quantize_mx(T.wq[:, o:o + 256], T.ws[:, o:o + 256], T.wb[:, 0:1024]).then_inc(S.qw1, 1)
    v.wait_ge(S.ldx, 16)
    v.quantize_mx(T.xq[:], T.xs[:], T.xb[:]).then_inc(S.qx, 1)

    def there(k, names):
        r = order[k]
        if r == rank:
            for s in (S.qw1, S.qw2, S.qx):
                t.wait_ge(s, 1)
        for part, n in gets.get(r, ()):
            if part in names:
                t.wait_ge(S["a%d%s" % (r, part)], n)

    def zmm(k, i):
        there(k, ("A0", "A", "C", "S") if i == 0 else ("A1", "A", "C", "S"))
        if k >= 3:
            t.wait_ge(S["ha%d" % (k - 3)], 4)
        b = 1024 * (k % 3) + 512 * i
        w = WC * order[k] + 128 * i
        t.matmul_mx(T.zp[:, b:b + NC], T.wq[:, w:w + 128], T.ws[:, w:w + 128], T.xq[:], T.xs[:],
                    True, True).then_inc(S["%s%d" % ("za" if i == 0 else "zb", k)], 1)

    def ymm(k):
        there(k, ("B", "C", "S"))
        t.wait_ge(S["hq%d" % k], 1)
        w = WC * order[k] + 256
        mm = t.matmul_mx(T.yp[:, 0:NC], T.wq[:, w:w + 128], T.ws[:, w:w + 128],
                         T.hq[:, NC * k:NC * k + NC], T.hs[:, NC * k:NC * k + NC], k == 0, k == N - 1)
        if k == N - 1:
            mm.then_inc(S.ydone, 1)

    for k in range(N - 2):
        zmm(k, 0)
        zmm(k, 1)
        if k >= 3:
            ymm(k - 3)
    zmm(N - 2, 1)
    ymm(N - 5)
    zmm(N - 1, 1)
    ymm(N - 4)
    zmm(N - 2, 0)
    zmm(N - 1, 0)
    ymm(N - 3)
    ymm(N - 2)
    ymm(N - 1)

    def hcol(k, b):
        return T.h[:, 4 * NC * k + b:4 * NC * (k + 1):4]

    def zbank(k, i):
        b = 1024 * (k % 3) + 512 * i
        return T.zp[:, b:b + NC]

    for k, i in [(k, 1) for k in range(N)] + [(N - 1, 0)]:
        sc.wait_ge(S["%s%d" % ("za" if i == 0 else "zb", k)], 1)
        sc.activation(hcol(k, 2 * i), zbank(k, i), ActivationFunctionType.Relu, scale=CSC).then_inc(S["ha%d" % k], 1)
        sc.activation(hcol(k, 2 * i + 1), zbank(k, i), ActivationFunctionType.Relu,
                      scale=-CSC).then_inc(S["ha%d" % k], 1)
    for k in range(N):
        ha = S["ha%d" % k]
        if k < N - 1:
            v.wait_ge(S["za%d" % k], 1)
            v.tensor_scalar(hcol(k, 0), zbank(k, 0), 0.0, CSC, AluOpType.max, AluOpType.mult).then_inc(ha, 1)
            v.tensor_scalar(hcol(k, 1), zbank(k, 0), -CSC, 0.0, AluOpType.mult, AluOpType.max).then_inc(ha, 1)
        v.wait_ge(ha, 4)
        v.quantize_mx(T.hq[:, NC * k:NC * k + NC], T.hs[:, NC * k:NC * k + NC],
                      T.h[:, 4 * NC * k:4 * NC * (k + 1)]).then_inc(S["hq%d" % k], 1)
    v.wait_ge(S.ydone, 1)
    v.tensor_copy(T.yo[:], T.yp[:, 0:NC]).then_inc(S.ycp, 1)
    g.sync.wait_ge(S.ycp, 1)
    g.sync.dma_start(T.y[:, :], T.yo[:]).then_inc(S.st, 16)
    g.sync.wait_ge(S.st, 16)
